import numpy as np
import ml_dtypes


def mxq(x, axis, fmt="e4m3"):
    dtype, down = {"e4m3": (ml_dtypes.float8_e4m3fn, 7), "e5m2": (ml_dtypes.float8_e5m2, 14)}[fmt]
    v = np.moveaxis(np.asarray(x, np.float32).astype(ml_dtypes.bfloat16).astype(np.float64), axis, -1)
    blocks = v.reshape(v.shape[:-1] + (-1, 32))
    amax = np.abs(blocks).max(-1, keepdims=True)
    byte = np.maximum(np.where(amax > 0, np.frexp(amax)[1] - 1 + 127, 0) - down, 1)
    scale = np.exp2(byte - 127.0)
    codes = (blocks / scale).astype(np.float32).astype(dtype).astype(np.float64)
    return np.moveaxis((codes * scale).reshape(v.shape), -1, axis)


WIDE = False


def mx_kscale(k):
    if not WIDE:
        return np.ones(k)
    levels = np.array([10, -10, 5, -5, 0])
    if k % 512:
        return np.exp2(np.random.permutation(np.resize(levels, k // 32))).repeat(32)
    a = np.empty((k // 512, 16))
    for p in range(k // 512):
        a[p, :8] = np.random.permutation(np.resize(levels, 8))
        for g in range(8):
            far = levels[np.abs(levels - a[p, g]) >= 10]
            a[p, g + 8] = far[np.random.randint(len(far))]
    return np.exp2(a.ravel()).repeat(32)


BF16 = ml_dtypes.bfloat16


def bf(x):
    return np.asarray(x, np.float32).astype(BF16)


def f64(x):
    return np.asarray(x).astype(np.float64)

def planes(Y):
    n, m = Y.shape
    b = f64(bf(Y)).reshape(n // 32, 32, m)
    amax = np.abs(b).max(1)
    byte = np.clip(np.where(amax > 0, np.frexp(amax)[1] - 1 + 127 - 7, 1), 1, 254)
    codes = (b * np.exp2(127.0 - byte)[:, None, :]).reshape(n, m).astype(np.float32).astype(ml_dtypes.float8_e4m3fn).view(np.uint8)
    words = codes.reshape(n // 512, 128, 4, m).transpose(0, 1, 3, 2)
    return np.ascontiguousarray(words), np.ascontiguousarray(byte.astype(np.uint8).reshape(n // 512, 16, m))


P, N, K = 512, 512, 8


def setup_inputs():
    s = mx_kscale(N)
    return {"w": bf(np.random.standard_normal((P, N)) / np.sqrt(N) * s[None, :]),
            "c": bf(np.random.standard_normal((K, N, N)) / s[None, :, None] / s[None, None, :])}


def _pair_update(z, zd, y):
    zi = zd[:, None]
    zj = zd[None, :]
    num = z * y.T - 1.1 * zi * y
    den = 1.21 * zi * zj - z * z
    return num / den


def core(w, c):
    w = f64(w)
    n = w.shape[0]
    wq = mxq(w, 1, "e4m3")

    v = wq @ mxq(f64(c), 1, "e4m3")

    r = mxq(v, 2, "e4m3") @ wq.T

    d = np.sum(v * w[None, :, :], axis=-1)

    e = 0.5 * (r + np.swapaxes(r, 1, 2))

    z = np.sum(d[:, :, None] * d[:, None, :], axis=0)
    zd = np.sum(d * d, axis=0)

    y = np.sum(d[:, None, :] * e, axis=0)

    u = _pair_update(z, zd, y)

    idx = np.arange(n)
    on_diag = idx[:, None] == idx[None, :]
    return np.where(on_diag, np.zeros_like(u), u)


def reference(w, c):
    R_out = core(w, c)
    words, scales = planes(R_out)
    return R_out, words, scales

@@ -1,0 +1,406 @@
+from contextlib import ExitStack
+
+import concourse.mybir as mybir
+from concourse.masks import make_identity
+
+P = 128
+N = 512
+KM = 8
+T = 4
+FLOPS = 2 * 2 * KM * N * N * N
+
+F32 = mybir.dt.float32
+BF16 = mybir.dt.bfloat16
+U32 = mybir.dt.uint32
+I32 = mybir.dt.int32
+U8 = mybir.dt.uint8
+FP8X4 = mybir.dt.float8_e4m3fn_x4
+ALU = mybir.AluOpType
+ACT = mybir.ActivationFunctionType
+AX = mybir.AxisListType
+
+LE = 21
+LD = -3
+LC = 13
+QC = (10, 9)
+QV = (9, 15)
+DS = 29
+DT = 34
+ZB = 37
+TBANK = {"at": "x", "bt": "v"}
+ZT = (36, 39, 38, 42)
+DN = (38, 42, 40, 45)
+GT = (42, 49, 54, 53)
+BANKS = {"vt": 2, "v": 2, "e": 3, "x": 1}
+ZBANK = ("x", "v", "vt", "vt")
+SY = {0: (0, 1, 3), 1: (1,), 2: (1, 2, 3), 3: (1, 3), 4: (2,), 5: (0, 1), 6: (1,), 7: ()}
+WG = (1, 2)
+WT = (-2, -2, 3, 3)
+PT = (-1, 3, 3, 3)
+PEORD = ('e', 'vt', 'd')
+VORD = ('y', 'd', 'qc', 'qv', 'c')
+SORD = ('c', 'y', 'vt')
+C0 = 4
+CVEC = (6,)
+CGPS = (10, 11, 12, 14, 16, 19, 20, 21, 22, 23, 25, 28, 29)
+VC = (0, 0, 1, 1)
+
+
+def tile_dampedffdiagjointdiagonalizationupdate_x1_kernel(tc, w, c, out_0, out_1, out_2):
+    nc = tc.nc
+    with ExitStack() as ctx:
+        keep = ctx.enter_context(tc.tile_pool(name="keep", bufs=1))
+        ring = ctx.enter_context(tc.tile_pool(name="ring", bufs=4))
+        psum = ctx.enter_context(tc.psum_pool(name="psum", bufs=1))
+        ctx.enter_context(tc.manual_schedule())
+
+        def bank(tag):
+            b = psum.tile([P, N], F32, name="ps_" + tag, tag=tag, bufs=BANKS[tag])
+            return b
+
+        w_raw = keep.tile([P, T, N], BF16, name="w_raw", align_bytes=64)
+        w_hbm = w.rearrange("(p t) m -> p t m", t=T)
+        for h in range(2):
+            nc.sync.dma_start(out=w_raw[:, 2 * h:2 * h + 2, :], in_=w_hbm[:, 2 * h:2 * h + 2, :])
+        c_hbm = c.rearrange("k (p j) n -> k p j n", j=4)
+        c_raw = []
+        for k in range(KM):
+            craw = keep.tile([P, 4, N], BF16, name="c_raw%d" % k, align_bytes=64)
+            nc.sync.dma_start(out=craw[:], in_=c_hbm[k])
+            c_raw.append(craw)
+
+        ident = keep.tile([P, P], F32, name="ident")
+        make_identity(nc, ident[:])
+        one = keep.tile([P, 1], F32, name="one")
+        nc.gpsimd.memset(one[:], 1.0)
+        ident16 = keep.tile([P, P], BF16, name="ident16")
+        nc.gpsimd.tensor_copy(out=ident16[:], in_=ident[:])
+        d_all = keep.tile([P, T, KM], F32, name="d_all")
+        warm = keep.tile([P, 1], F32, name="warm")
+        nc.scalar.activation(out=warm[:], in_=one[:], func=ACT.Abs_reciprocal_sqrt)
+
+        w_g = keep.tile([P, 4 * N], BF16, name="w_g", align_bytes=64)
+        w_codes = keep.tile([P, N], U32, name="w_codes", align_bytes=64)
+        w_scales = keep.tile([P, N], U8, name="w_scales", align_bytes=64)
+        words = w_raw[:].rearrange("p t m -> p (t m)").bitcast(F32)
+        for h in range(2):
+            ps = bank("e")
+            for tt in range(2):
+                t = 2 * h + tt
+                for u in range(2):
+                    o = (2 * tt + u) * P
+                    nc.tensor.transpose(ps[:, o:o + P], words[:, 256 * t + u:256 * (t + 1):2], ident[:])
+            dst = w_g[:].bitcast(F32)[:, N * h:N * (h + 1)].rearrange("p (t r u) -> p t r u", t=2, u=2)
+            src = ps[:].rearrange("p (t u r) -> p t r u", t=2, u=2)
+            if h == 0:
+                nc.vector.tensor_copy(out=dst, in_=src)
+            else:
+                nc.scalar.copy(out=dst, in_=src)
+        c_g = {}
+        c_q = {}
+        v_g = {}
+        v_q = {}
+        y_acc = []
+        for t in range(T):
+            ya = keep.tile([P, N], F32, name="y_acc%d" % t)
+            y_acc.append(ya)
+
+        def c_interleave(k, t, eng):
+            if k not in c_g:
+                cg = ring.tile([P, 4 * N], BF16, name="c_g", tag="c_g", align_bytes=64)
+                c_g[k] = cg
+            dst = c_g[k][:, N * t:N * (t + 1)].rearrange("p (q j) -> p q j", j=4)
+            src = c_raw[k][:].rearrange("p j (q t) -> p t q j", t=T)[:, t]
+            if eng == "g":
+                nc.gpsimd.tensor_scalar(dst, src, 1.0, 0.0, op0=ALU.mult, op1=ALU.add)
+            elif eng == "v":
+                nc.vector.tensor_copy(out=dst, in_=src)
+            else:
+                nc.scalar.copy(out=dst, in_=src)
+
+        def c_quantize(k, h):
+            if k not in c_q:
+                cc = ring.tile([P, N], U32, name="c_codes", tag="c_codes", align_bytes=64)
+                cs = ring.tile([P, N], U8, name="c_scales", tag="c_scales", align_bytes=64)
+                c_q[k] = (cc, cs)
+            cols = slice(256 * h, 256 * (h + 1))
+            nc.vector.quantize_mx(out=c_q[k][0][:, cols].bitcast(FP8X4), scales=c_q[k][1][:, cols],
+                                  in_=c_g[k][:, 1024 * h:1024 * (h + 1)])
+
+        def mm(ps, lhs, lcols, rhs, rcols, start=True, stop=True):
+            nc.tensor.matmul_mx(
+                out=ps,
+                lhsT=lhs[0][:, lcols].bitcast(FP8X4), lhsT_scale=lhs[1][:, lcols],
+                rhs=rhs[0][:, rcols].bitcast(FP8X4), rhs_scale=rhs[1][:, rcols],
+                start=start, stop=stop)
+
+        wq = (w_codes, w_scales)
+        full = slice(0, N)
+
+        def blk(t):
+            return slice(P * t, P * (t + 1))
+
+        vt_ps = {}
+        v_ps = {}
+        e_ps = {}
+
+        def vt_mm(i):
+            k, g = divmod(i, T)
+            ps = bank("vt")
+            for t in range(T):
+                mm(ps[:, blk(t)], c_q[k], blk(t), wq, blk(g))
+            vt_ps[i] = ps
+
+        def vt_out(i):
+            k, g = divmod(i, T)
+            if k not in v_g:
+                vg = ring.tile([P, 4 * N], BF16, name="v_g", tag="v_g", align_bytes=64)
+                v_g[k] = vg
+            nc.scalar.copy(out=v_g[k][:, N * g:N * (g + 1)].rearrange("p (i t) -> p i t", t=T),
+                           in_=vt_ps[i][:].rearrange("p (t i) -> p i t", t=T))
+
+        def v_quantize(k, h):
+            if h == 0:
+                vc = ring.tile([P, N], U32, name="v_codes", tag="v_codes", align_bytes=64)
+                vs = ring.tile([P, N], U8, name="v_scales", tag="v_scales", align_bytes=64)
+                v_q[k] = (vc, vs)
+            cols = slice(256 * h, 256 * (h + 1))
+            nc.vector.quantize_mx(out=v_q[k][0][:, cols].bitcast(FP8X4), scales=v_q[k][1][:, cols],
+                                  in_=v_g[k][:, 1024 * h:1024 * (h + 1)])
+
+        def d_mm(j):
+            k, t = divmod(j, T)
+            ps = bank("v")
+            mm(ps[:], wq, blk(t), c_q[k], full)
+            v_ps[j] = ps
+
+        def d_out(j):
+            k, t = divmod(j, T)
+            junk = ring.tile([P, N], F32, name="junk", tag="junk")
+            nc.vector.scalar_tensor_tensor(
+                out=junk[:].rearrange("p (s q) -> p s q", s=T),
+                in0=v_ps[j][:].rearrange("p (s q) -> p s q", s=T), scalar=1.0,
+                in1=w_raw[:, t, :].rearrange("p (q s) -> p s q", s=T),
+                op0=ALU.mult, op1=ALU.mult, accum_out=d_all[:, t, k:k + 1])
+
+        def e_mm(e):
+            k, t = divmod(e, T)
+            ps = bank("e")
+            mm(ps[:], v_q[k], blk(t), wq, full, True, False)
+            mm(ps[:], wq, blk(t), v_q[k], full, False, True)
+            e_ps[e] = ps
+
+        def e_out(e):
+            k, t = divmod(e, T)
+            ps = e_ps[e]
+            dcol = d_all[:, t, k:k + 1]
+            if t in SY[k]:
+                tmp = y_acc[t]
+                if k > 0:
+                    tmp = ring.tile([P, N], F32, name="y_tmp", tag="y_tmp")
+                nc.scalar.activation(out=tmp[:], in_=ps[:], func=ACT.Copy, scale=dcol)
+                if k > 0:
+                    nc.gpsimd.tensor_tensor(out=y_acc[t][:], in0=y_acc[t][:], in1=tmp[:], op=ALU.add)
+            elif k == 0:
+                nc.vector.tensor_scalar_mul(y_acc[t][:], ps[:], dcol)
+            else:
+                nc.vector.scalar_tensor_tensor(out=y_acc[t][:], in0=ps[:], scalar=dcol, in1=y_acc[t][:],
+                                               op0=ALU.mult, op1=ALU.add)
+
+        tail = {}
+        z_ps = {}
+        zz = {}
+        den = {}
+        gg = {}
+        w_y = {}
+        p_y = {}
+
+        split_a = keep.tile([P, T, P], BF16, name="split_a", align_bytes=64)
+        split_b = keep.tile([P, T, P], BF16, name="split_b", align_bytes=64)
+        nc.gpsimd.memset(split_a[:], 0.0)
+        nc.gpsimd.memset(split_b[:], 0.0)
+
+        def d_split():
+            ones3 = [P, T, 3, KM]
+            d = d_all[:]
+            av = split_a[:, :, 0:9 * KM].rearrange("p t (a b k) -> p t a b k", a=3, b=3)
+            bv = split_b[:, :, 0:9 * KM].rearrange("p t (a b k) -> p t a b k", a=3, b=3)
+            rest = d
+            for a in range(3):
+                nc.vector.tensor_copy(out=av[:, :, a], in_=rest.unsqueeze(2).to_broadcast(ones3))
+                nc.gpsimd.tensor_copy(out=bv[:, :, :, a, :], in_=av[:, :, a])
+                if a < 2:
+                    r = keep.tile([P, T, KM], F32, name="d_rest%d" % a)
+                    nc.vector.tensor_tensor(out=r[:], in0=rest, in1=av[:, :, a, 0, :], op=ALU.subtract)
+                    rest = r[:]
+            d2 = keep.tile([P, T, KM], F32, name="d2")
+            zd = keep.tile([P, T], F32, name="zd")
+            zs = keep.tile([P, T], F32, name="zs")
+            ys = keep.tile([P, T], F32, name="ys")
+            nc.vector.tensor_tensor(out=d2[:], in0=d, in1=d, op=ALU.mult)
+            nc.vector.tensor_reduce(out=zd[:], in_=d2[:], axis=AX.X, op=ALU.add)
+            nc.vector.tensor_scalar_mul(zs[:], zd[:], 1.21)
+            nc.vector.tensor_scalar_mul(ys[:], zd[:], -1.1)
+            tail["zd"], tail["zs"], tail["ys"] = zd, zs, ys
+
+        def d_turn():
+            assert "zd" in tail
+            for name, src, eng in (("at", split_a, nc.vector.tensor_copy), ("bt", split_b, nc.scalar.copy)):
+                ps = psum.tile([P, N], BF16, name="ps_" + name, tag=TBANK[name], bufs=BANKS[TBANK[name]])
+                for t in range(T):
+                    nc.tensor.transpose(ps[:, blk(t)], src[:, t, :], ident16[:])
+                s = keep.tile([P, N], BF16, name=name, align_bytes=64)
+                eng(out=s[:], in_=ps[:])
+                tail[name] = s
+
+        def zdb_pass():
+            ps = bank("v")
+            for t in range(T):
+                nc.tensor.matmul(ps[:, blk(t)], lhsT=tail["zd"][:, t:t + 1].to_broadcast([P, P]), rhs=ident[:],
+                                 start=True, stop=True)
+            tail["zdb"] = ps
+
+        def z_pass(t):
+            ps = bank(ZBANK[t])
+            nc.tensor.matmul(ps[:], lhsT=tail["at"][:, blk(t)], rhs=tail["bt"][:], start=True, stop=True)
+            z_ps[t] = ps
+
+        def zz_pass(t):
+            a = keep.tile([P, N], F32, name="zz%d" % t)
+            nc.scalar.activation(out=a[:], in_=z_ps[t][:], func=ACT.Square)
+            zz[t] = a
+
+        def den_pass(t):
+            a = keep.tile([P, N], F32, name="den%d" % t)
+            nc.vector.scalar_tensor_tensor(out=a[:], in0=tail["zdb"][:], scalar=tail["zs"][:, t:t + 1], in1=zz[t][:],
+                                           op0=ALU.mult, op1=ALU.subtract)
+            den[t] = a
+
+        def gg_pass(t):
+            r = keep.tile([P, N], F32, name="rs%d" % t)
+            nc.scalar.activation(out=r[:], in_=den[t][:], func=ACT.Abs_reciprocal_sqrt, scale=2.0)
+            a = keep.tile([P, N], F32, name="gg%d" % t)
+            nc.scalar.activation(out=a[:], in_=r[:], func=ACT.Square)
+            nc.gpsimd.affine_select(out=a[:, blk(t)], in_=a[:, blk(t)], pattern=[[1, P]], compare_op=ALU.not_equal,
+                                    fill=0.0, base=0, channel_multiplier=-1)
+            gg[t] = a
+
+        def w_pass(t):
+            a = keep.tile([P, N], F32, name="w_y%d" % t)
+            eng = nc.gpsimd if t in WG else nc.vector
+            eng.tensor_tensor(out=a[:], in0=y_acc[t][:], in1=gg[t][:], op=ALU.mult)
+            w_y[t] = a
+
+        def p_pass(t):
+            a = keep.tile([P, N], F32, name="p_y%d" % t)
+            nc.vector.tensor_tensor(out=a[:], in0=z_ps[t][:], in1=w_y[t][:], op=ALU.mult)
+            p_y[t] = a
+
+        for t in range(T):
+            c_interleave(0, t, "v" if t < C0 else "s")
+        nc.vector.quantize_mx(out=w_codes[:].bitcast(FP8X4), scales=w_scales[:], in_=w_g[:])
+        c_quantize(0, 0)
+        c_quantize(0, 1)
+        i0 = min(LD, T - max(QC))
+        for n in range(T, LC + i0):
+            c_interleave(n // T, n % T, "v" if n in CVEC else "g" if n in CGPS else "s")
+
+        END = T * KM
+        assert all(WT[t] >= t - T and PT[t] >= WT[t] for t in range(T))
+        for i in range(i0, END + LE + 4):
+            e = i - LE
+            j = i - LD
+            vt_on, e_on, d_on = 0 <= i < END, 0 <= e < END, 0 <= j < END
+            for what in PEORD:
+                if what == "vt" and vt_on:
+                    vt_mm(i)
+                if what == "e" and e_on:
+                    e_mm(e)
+                if what == "d" and d_on:
+                    d_mm(j)
+            s_y = e_on and (e % T) in SY[e // T]
+            for what in SORD:
+                if what == "vt" and vt_on:
+                    vt_out(i)
+                if what == "y" and s_y:
+                    e_out(e)
+                n = i + LC
+                if what == "c" and T <= n < END and n >= LC + i0 and n not in CVEC:
+                    c_interleave(n // T, n % T, "g" if n in CGPS else "s")
+            for what in VORD:
+                if what == "y" and e_on and not s_y:
+                    e_out(e)
+                if what == "d" and d_on:
+                    d_out(j)
+                n = i + LC
+                if what == "c" and T <= n < END and n in CVEC:
+                    c_interleave(n // T, n % T, "v")
+                if what == "qc":
+                    for h in range(2):
+                        n = i + QC[h]
+                        if n % T == 0 and T <= n < END:
+                            c_quantize(n // T, h)
+                if what == "qv":
+                    for h in range(2):
+                        n = i - QV[h]
+                        if n % T == 0 and 0 <= n < END:
+                            v_quantize(n // T, h)
+            if i == DS:
+                d_split()
+            if i == DT:
+                d_turn()
+            if i == ZB:
+                zdb_pass()
+            for t in range(T):
+                if i == ZT[t]:
+                    z_pass(t)
+                    zz_pass(t)
+                if i == DN[t]:
+                    den_pass(t)
+                if i == GT[t]:
+                    gg_pass(t)
+            for t in range(T):
+                if e == END + WT[t]:
+                    w_pass(t)
+            for t in range(T):
+                if e == END + PT[t]:
+                    p_pass(t)
+
+        ty_ps = []
+        u_all = keep.tile([P, T, N], F32, name="u_all")
+        u_g = keep.tile([P, 4 * N], BF16, name="u_g", align_bytes=64)
+        o_codes = keep.tile([P, N], U32, name="o_codes", align_bytes=64)
+        o_scales = keep.tile([P, N], U8, name="o_scales", align_bytes=64)
+        o0 = out_0.rearrange("(p t) m -> p t m", t=T)
+        o1 = out_1.rearrange("g p m t -> (g p) (m t)").bitcast(I32)
+        o2 = out_2.rearrange("g q m -> (g q) m").bitcast(I32)
+
+        for t in range(T):
+            ps = bank("e" if t < 3 else "v")
+            for t2 in range(T):
+                nc.tensor.transpose(ps[:, blk(t2)], w_y[t2][:, blk(t)], ident[:])
+            ty_ps.append(ps)
+        for h in range(2):
+            cols = slice(256 * h, 256 * (h + 1))
+            qs = slice(64 * h, 64 * (h + 1))
+            for t in range(T):
+                nc.vector.scalar_tensor_tensor(out=u_all[:, t, cols].rearrange("p (q s) -> p q s", s=T),
+                                               in0=ty_ps[t][:].rearrange("p (s q) -> p q s", s=T)[:, qs],
+                                               scalar=tail["ys"][:, t:t + 1],
+                                               in1=p_y[t][:].rearrange("p (s q) -> p q s", s=T)[:, qs],
+                                               op0=ALU.mult, op1=ALU.add)
+            nc.sync.dma_start(out=o0[:, :, cols], in_=u_all[:, :, cols])
+            dst = u_g[:, 1024 * h:1024 * (h + 1)].rearrange("p (m t) -> p m t", t=T)
+            src = u_all[:, :, cols].rearrange("p t m -> p m t")
+            if h == 0:
+                nc.scalar.copy(out=dst, in_=src)
+            else:
+                nc.vector.tensor_copy(out=dst, in_=src)
+        for h in range(2):
+            cols = slice(256 * h, 256 * (h + 1))
+            nc.vector.quantize_mx(out=o_codes[:, cols].bitcast(FP8X4), scales=o_scales[:, cols],
+                                  in_=u_g[:, 1024 * h:1024 * (h + 1)])
+            nc.sync.dma_start(out=o1[:, cols], in_=o_codes[:, cols].bitcast(I32))
+        for b in range(4):
+            eng = (nc.scalar, nc.gpsimd, nc.scalar, nc.sync)[b]
+            eng.dma_start(out=o2[4 * b:4 * b + 4, :], in_=o_scales[32 * b:32 * b + 4, :].bitcast(I32))

@@ -19,30 +19,30 @@ ALU = mybir.AluOpType
 ACT = mybir.ActivationFunctionType
 AX = mybir.AxisListType
 
-LE = 21
+LE = 18
 LD = -3
-LC = 13
-QC = (10, 9)
-QV = (9, 15)
-DS = 29
-DT = 34
-ZB = 37
+LC = 15
+QC = (8, 7)
+QV = (11, 13)
+DS = 28
+DT = 33
+ZB = 34
 TBANK = {"at": "x", "bt": "v"}
-ZT = (36, 39, 38, 42)
-DN = (38, 42, 40, 45)
-GT = (42, 49, 54, 53)
+ZT = (36, 40, 41, 38)
+DN = (39, 42, 42, 45)
+GT = (44, 50, 46, 48)
 BANKS = {"vt": 2, "v": 2, "e": 3, "x": 1}
 ZBANK = ("x", "v", "vt", "vt")
-SY = {0: (0, 1, 3), 1: (1,), 2: (1, 2, 3), 3: (1, 3), 4: (2,), 5: (0, 1), 6: (1,), 7: ()}
-WG = (1, 2)
-WT = (-2, -2, 3, 3)
-PT = (-1, 3, 3, 3)
-PEORD = ('e', 'vt', 'd')
-VORD = ('y', 'd', 'qc', 'qv', 'c')
-SORD = ('c', 'y', 'vt')
+SY = {0: (0, 1, 3), 1: (0, 1, 2, 3), 2: (0, 1, 2, 3), 3: (0, 1, 3), 4: (1, 3), 5: (1, 2), 6: (0,), 7: (2,)}
+WG = (1,)
+WT = (-4, 0, 0, 0)
+PT = (1, 2, 0, 0)
+PEORD = ('vt', 'e', 'd')
+VORD = ('qv', 'd', 'qc', 'y', 'c')
+SORD = ('vt', 'c', 'y')
 C0 = 4
-CVEC = (6,)
-CGPS = (10, 11, 12, 14, 16, 19, 20, 21, 22, 23, 25, 28, 29)
+CVEC = (5, 7, 9, 12, 13, 19, 22, 24, 29, 30)
+CGPS = ()
 VC = (0, 0, 1, 1)
 
 
@@ -79,10 +79,17 @@ def tile_dampedffdiagjointdiagonalizationupdate_x1_kernel(tc, w, c, out_0, out_1
         warm = keep.tile([P, 1], F32, name="warm")
         nc.scalar.activation(out=warm[:], in_=one[:], func=ACT.Abs_reciprocal_sqrt)
 
+        def w_permute(t):
+            nc.scalar.copy(out=w_perm[:, t, :].rearrange("p (s q) -> p s q", s=T),
+                           in_=w_raw[:, t, :].rearrange("p (q s) -> p s q", s=T))
+
         w_g = keep.tile([P, 4 * N], BF16, name="w_g", align_bytes=64)
         w_codes = keep.tile([P, N], U32, name="w_codes", align_bytes=64)
         w_scales = keep.tile([P, N], U8, name="w_scales", align_bytes=64)
         words = w_raw[:].rearrange("p t m -> p (t m)").bitcast(F32)
+        w_perm = keep.tile([P, T, N], BF16, name="w_perm", align_bytes=64)
+        for t in range(2):
+            w_permute(t)
         for h in range(2):
             ps = bank("e")
             for tt in range(2):
@@ -109,12 +116,13 @@ def tile_dampedffdiagjointdiagonalizationupdate_x1_kernel(tc, w, c, out_0, out_1
             if k not in c_g:
                 cg = ring.tile([P, 4 * N], BF16, name="c_g", tag="c_g", align_bytes=64)
                 c_g[k] = cg
-            dst = c_g[k][:, N * t:N * (t + 1)].rearrange("p (q j) -> p q j", j=4)
-            src = c_raw[k][:].rearrange("p j (q t) -> p t q j", t=T)[:, t]
-            if eng == "g":
+            dst = c_g[k][:].rearrange("p (t q j) -> p q t j", t=T, j=4)[:, 32 * t:32 * t + 32]
+            src = c_raw[k][:].rearrange("p j (q t) -> p q t j", t=T)[:, 32 * t:32 * t + 32]
+            if eng == "v":
+                for h in range(2):
+                    nc.vector.tensor_copy(out=dst[:, :, 2 * h:2 * h + 2], in_=src[:, :, 2 * h:2 * h + 2])
+            elif eng == "g":
                 nc.gpsimd.tensor_scalar(dst, src, 1.0, 0.0, op0=ALU.mult, op1=ALU.add)
-            elif eng == "v":
-                nc.vector.tensor_copy(out=dst, in_=src)
             else:
                 nc.scalar.copy(out=dst, in_=src)
 
@@ -178,9 +186,7 @@ def tile_dampedffdiagjointdiagonalizationupdate_x1_kernel(tc, w, c, out_0, out_1
             k, t = divmod(j, T)
             junk = ring.tile([P, N], F32, name="junk", tag="junk")
             nc.vector.scalar_tensor_tensor(
-                out=junk[:].rearrange("p (s q) -> p s q", s=T),
-                in0=v_ps[j][:].rearrange("p (s q) -> p s q", s=T), scalar=1.0,
-                in1=w_raw[:, t, :].rearrange("p (q s) -> p s q", s=T),
+                out=junk[:], in0=v_ps[j][:], scalar=1.0, in1=w_perm[:, t, :],
                 op0=ALU.mult, op1=ALU.mult, accum_out=d_all[:, t, k:k + 1])
 
         def e_mm(e):
@@ -301,6 +307,8 @@ def tile_dampedffdiagjointdiagonalizationupdate_x1_kernel(tc, w, c, out_0, out_1
         nc.vector.quantize_mx(out=w_codes[:].bitcast(FP8X4), scales=w_scales[:], in_=w_g[:])
         c_quantize(0, 0)
         c_quantize(0, 1)
+        w_permute(2)
+        w_permute(3)
         i0 = min(LD, T - max(QC))
         for n in range(T, LC + i0):
             c_interleave(n // T, n % T, "v" if n in CVEC else "g" if n in CGPS else "s")

@@ -19,29 +19,33 @@ ALU = mybir.AluOpType
 ACT = mybir.ActivationFunctionType
 AX = mybir.AxisListType
 
-LE = 18
-LD = -3
-LC = 15
-QC = (8, 7)
-QV = (11, 13)
-DS = 28
-DT = 33
-ZB = 34
+LE = 21
+LD = -2
+LC = 10
+QC = (6, 4)
+QV = (13, 14)
+DS = 29
+RD = 34
+DT = 36
+DC = 36
+ZZ = (42, 42, 43, 42)
+ZB = 42
 TBANK = {"at": "x", "bt": "v"}
-ZT = (36, 40, 41, 38)
-DN = (39, 42, 42, 45)
-GT = (44, 50, 46, 48)
+ZT = (40, 42, 40, 40)
+DN = (43, 43, 46, 46)
+GT = (47, 45, 50, 47)
+GL = (16, 53, 56, 53)
 BANKS = {"vt": 2, "v": 2, "e": 3, "x": 1}
 ZBANK = ("x", "v", "vt", "vt")
-SY = {0: (0, 1, 3), 1: (0, 1, 2, 3), 2: (0, 1, 2, 3), 3: (0, 1, 3), 4: (1, 3), 5: (1, 2), 6: (0,), 7: (2,)}
-WG = (1,)
-WT = (-4, 0, 0, 0)
-PT = (1, 2, 0, 0)
-PEORD = ('vt', 'e', 'd')
-VORD = ('qv', 'd', 'qc', 'y', 'c')
-SORD = ('vt', 'c', 'y')
+SY = {0: (1, 2), 1: (0, 1, 2), 2: (), 3: (1,), 4: (0, 1, 3), 5: (0, 2), 6: (1,), 7: ()}
+WG = (1, 2, 3)
+WT = (-2, 3, 3, 3)
+PT = (0, 3, 3, 3)
+PEORD = ('e', 'vt', 'd')
+VORD = ('c', 'y', 'qv', 'qc', 'd')
+SORD = ('c', 'vt', 'y')
 C0 = 4
-CVEC = (5, 7, 9, 12, 13, 19, 22, 24, 29, 30)
+CVEC = (4, 6, 10, 12, 14, 18, 21, 28)
 CGPS = ()
 VC = (0, 0, 1, 1)
 
@@ -218,6 +222,7 @@ def tile_dampedffdiagjointdiagonalizationupdate_x1_kernel(tc, w, c, out_0, out_1
         zz = {}
         den = {}
         gg = {}
+        gl = {}
         w_y = {}
         p_y = {}
 
@@ -233,30 +238,38 @@ def tile_dampedffdiagjointdiagonalizationupdate_x1_kernel(tc, w, c, out_0, out_1
             bv = split_b[:, :, 0:9 * KM].rearrange("p t (a b k) -> p t a b k", a=3, b=3)
             rest = d
             for a in range(3):
-                nc.vector.tensor_copy(out=av[:, :, a], in_=rest.unsqueeze(2).to_broadcast(ones3))
-                nc.gpsimd.tensor_copy(out=bv[:, :, :, a, :], in_=av[:, :, a])
+                nc.gpsimd.tensor_scalar(av[:, :, a], rest.unsqueeze(2).to_broadcast(ones3), 1.0, 0.0, op0=ALU.mult, op1=ALU.add)
                 if a < 2:
                     r = keep.tile([P, T, KM], F32, name="d_rest%d" % a)
-                    nc.vector.tensor_tensor(out=r[:], in0=rest, in1=av[:, :, a, 0, :], op=ALU.subtract)
+                    nc.gpsimd.tensor_tensor(out=r[:], in0=rest, in1=av[:, :, a, 0, :], op=ALU.subtract)
                     rest = r[:]
+            for a in range(3):
+                nc.gpsimd.tensor_scalar(bv[:, :, :, a, :], av[:, :, a], 1.0, 0.0, op0=ALU.mult, op1=ALU.add)
             d2 = keep.tile([P, T, KM], F32, name="d2")
+            nc.gpsimd.tensor_tensor(out=d2[:], in0=d, in1=d, op=ALU.mult)
+            tail["d2"] = d2
+
+        def zd_pass():
             zd = keep.tile([P, T], F32, name="zd")
             zs = keep.tile([P, T], F32, name="zs")
             ys = keep.tile([P, T], F32, name="ys")
-            nc.vector.tensor_tensor(out=d2[:], in0=d, in1=d, op=ALU.mult)
-            nc.vector.tensor_reduce(out=zd[:], in_=d2[:], axis=AX.X, op=ALU.add)
-            nc.vector.tensor_scalar_mul(zs[:], zd[:], 1.21)
-            nc.vector.tensor_scalar_mul(ys[:], zd[:], -1.1)
+            nc.vector.tensor_reduce(out=zd[:], in_=tail["d2"][:], axis=AX.X, op=ALU.add)
+            nc.gpsimd.tensor_scalar(zs[:], zd[:], 1.21, 0.0, op0=ALU.mult, op1=ALU.add)
+            nc.gpsimd.tensor_scalar(ys[:], zd[:], -1.1, 0.0, op0=ALU.mult, op1=ALU.add)
             tail["zd"], tail["zs"], tail["ys"] = zd, zs, ys
 
         def d_turn():
-            assert "zd" in tail
-            for name, src, eng in (("at", split_a, nc.vector.tensor_copy), ("bt", split_b, nc.scalar.copy)):
+            assert "d2" in tail
+            for name, src in (("at", split_a), ("bt", split_b)):
                 ps = psum.tile([P, N], BF16, name="ps_" + name, tag=TBANK[name], bufs=BANKS[TBANK[name]])
                 for t in range(T):
                     nc.tensor.transpose(ps[:, blk(t)], src[:, t, :], ident16[:])
+                tail[name + "_ps"] = ps
+
+        def d_copy():
+            for name, eng in (("at", nc.vector.tensor_copy), ("bt", nc.scalar.copy)):
                 s = keep.tile([P, N], BF16, name=name, align_bytes=64)
-                eng(out=s[:], in_=ps[:])
+                eng(out=s[:], in_=tail[name + "_ps"][:])
                 tail[name] = s
 
         def zdb_pass():
@@ -273,28 +286,40 @@ def tile_dampedffdiagjointdiagonalizationupdate_x1_kernel(tc, w, c, out_0, out_1
 
         def zz_pass(t):
             a = keep.tile([P, N], F32, name="zz%d" % t)
-            nc.scalar.activation(out=a[:], in_=z_ps[t][:], func=ACT.Square)
+            nc.scalar.activation(out=a[:, P * t:], in_=z_ps[t][:, P * t:], func=ACT.Square)
             zz[t] = a
 
         def den_pass(t):
             a = keep.tile([P, N], F32, name="den%d" % t)
-            nc.vector.scalar_tensor_tensor(out=a[:], in0=tail["zdb"][:], scalar=tail["zs"][:, t:t + 1], in1=zz[t][:],
-                                           op0=ALU.mult, op1=ALU.subtract)
+            nc.vector.scalar_tensor_tensor(out=a[:, P * t:], in0=tail["zdb"][:, P * t:], scalar=tail["zs"][:, t:t + 1],
+                                           in1=zz[t][:, P * t:], op0=ALU.mult, op1=ALU.subtract)
             den[t] = a
 
         def gg_pass(t):
             r = keep.tile([P, N], F32, name="rs%d" % t)
-            nc.scalar.activation(out=r[:], in_=den[t][:], func=ACT.Abs_reciprocal_sqrt, scale=2.0)
+            nc.scalar.activation(out=r[:, P * t:], in_=den[t][:, P * t:], func=ACT.Abs_reciprocal_sqrt, scale=2.0)
             a = keep.tile([P, N], F32, name="gg%d" % t)
-            nc.scalar.activation(out=a[:], in_=r[:], func=ACT.Square)
+            nc.scalar.activation(out=a[:, P * t:], in_=r[:, P * t:], func=ACT.Square)
             nc.gpsimd.affine_select(out=a[:, blk(t)], in_=a[:, blk(t)], pattern=[[1, P]], compare_op=ALU.not_equal,
                                     fill=0.0, base=0, channel_multiplier=-1)
             gg[t] = a
 
+        def gl_pass(t):
+            if t == 2:
+                ps, o = gl[1][0], P
+            else:
+                ps, o = bank("e" if t == 1 else "v"), 0
+            for t2 in range(t):
+                nc.tensor.transpose(ps[:, o + P * t2:o + P * t2 + P], gg[t2][:, blk(t)], ident[:])
+            gl[t] = (ps, o)
+
         def w_pass(t):
             a = keep.tile([P, N], F32, name="w_y%d" % t)
             eng = nc.gpsimd if t in WG else nc.vector
-            eng.tensor_tensor(out=a[:], in0=y_acc[t][:], in1=gg[t][:], op=ALU.mult)
+            eng.tensor_tensor(out=a[:, P * t:], in0=y_acc[t][:, P * t:], in1=gg[t][:, P * t:], op=ALU.mult)
+            if t > 0:
+                ps, o = gl[t]
+                nc.vector.tensor_tensor(out=a[:, :P * t], in0=ps[:, o:o + P * t], in1=y_acc[t][:, :P * t], op=ALU.mult)
             w_y[t] = a
 
         def p_pass(t):
@@ -355,18 +380,26 @@ def tile_dampedffdiagjointdiagonalizationupdate_x1_kernel(tc, w, c, out_0, out_1
                             v_quantize(n // T, h)
             if i == DS:
                 d_split()
+            if i == RD:
+                zd_pass()
             if i == DT:
                 d_turn()
+            if i == DC:
+                d_copy()
             if i == ZB:
                 zdb_pass()
             for t in range(T):
                 if i == ZT[t]:
                     z_pass(t)
+                if i == ZZ[t]:
                     zz_pass(t)
                 if i == DN[t]:
                     den_pass(t)
                 if i == GT[t]:
                     gg_pass(t)
+            for t in range(1, T):
+                if i == GL[t]:
+                    gl_pass(t)
             for t in range(T):
                 if e == END + WT[t]:
                     w_pass(t)

from contextlib import ExitStack

import concourse.mybir as mybir
from concourse.masks import make_identity

P = 128
N = 512
KM = 8
T = 4
FLOPS = 2 * 2 * KM * N * N * N

F32 = mybir.dt.float32
BF16 = mybir.dt.bfloat16
U32 = mybir.dt.uint32
I32 = mybir.dt.int32
U8 = mybir.dt.uint8
FP8X4 = mybir.dt.float8_e4m3fn_x4
ALU = mybir.AluOpType
ACT = mybir.ActivationFunctionType
AX = mybir.AxisListType

LE = 21
LD = -2
LC = 10
QC = (6, 4)
QV = (13, 14)
DS = 29
RD = 34
DT = 36
DC = 36
ZZ = (42, 42, 43, 42)
ZB = 42
TBANK = {"at": "x", "bt": "v"}
ZT = (40, 42, 40, 40)
DN = (43, 43, 46, 46)
GT = (47, 45, 50, 47)
GL = (16, 53, 56, 53)
BANKS = {"vt": 2, "v": 2, "e": 3, "x": 1}
ZBANK = ("x", "v", "vt", "vt")
SY = {0: (1, 2), 1: (0, 1, 2), 2: (), 3: (1,), 4: (0, 1, 3), 5: (0, 2), 6: (1,), 7: ()}
WG = (1, 2, 3)
WT = (-2, 3, 3, 3)
PT = (0, 3, 3, 3)
PEORD = ('e', 'vt', 'd')
VORD = ('c', 'y', 'qv', 'qc', 'd')
SORD = ('c', 'vt', 'y')
C0 = 4
CVEC = (4, 6, 10, 12, 14, 18, 21, 28)
CGPS = ()
VC = (0, 0, 1, 1)


def tile_dampedffdiagjointdiagonalizationupdate_x1_kernel(tc, w, c, out_0, out_1, out_2):
    nc = tc.nc
    with ExitStack() as ctx:
        keep = ctx.enter_context(tc.tile_pool(name="keep", bufs=1))
        ring = ctx.enter_context(tc.tile_pool(name="ring", bufs=4))
        psum = ctx.enter_context(tc.psum_pool(name="psum", bufs=1))
        ctx.enter_context(tc.manual_schedule())

        def bank(tag):
            b = psum.tile([P, N], F32, name="ps_" + tag, tag=tag, bufs=BANKS[tag])
            return b

        w_raw = keep.tile([P, T, N], BF16, name="w_raw", align_bytes=64)
        w_hbm = w.rearrange("(p t) m -> p t m", t=T)
        for h in range(2):
            nc.sync.dma_start(out=w_raw[:, 2 * h:2 * h + 2, :], in_=w_hbm[:, 2 * h:2 * h + 2, :])
        c_hbm = c.rearrange("k (p j) n -> k p j n", j=4)
        c_raw = []
        for k in range(KM):
            craw = keep.tile([P, 4, N], BF16, name="c_raw%d" % k, align_bytes=64)
            nc.sync.dma_start(out=craw[:], in_=c_hbm[k])
            c_raw.append(craw)

        ident = keep.tile([P, P], F32, name="ident")
        make_identity(nc, ident[:])
        one = keep.tile([P, 1], F32, name="one")
        nc.gpsimd.memset(one[:], 1.0)
        ident16 = keep.tile([P, P], BF16, name="ident16")
        nc.gpsimd.tensor_copy(out=ident16[:], in_=ident[:])
        d_all = keep.tile([P, T, KM], F32, name="d_all")
        warm = keep.tile([P, 1], F32, name="warm")
        nc.scalar.activation(out=warm[:], in_=one[:], func=ACT.Abs_reciprocal_sqrt)

        def w_permute(t):
            nc.scalar.copy(out=w_perm[:, t, :].rearrange("p (s q) -> p s q", s=T),
                           in_=w_raw[:, t, :].rearrange("p (q s) -> p s q", s=T))

        w_g = keep.tile([P, 4 * N], BF16, name="w_g", align_bytes=64)
        w_codes = keep.tile([P, N], U32, name="w_codes", align_bytes=64)
        w_scales = keep.tile([P, N], U8, name="w_scales", align_bytes=64)
        words = w_raw[:].rearrange("p t m -> p (t m)").bitcast(F32)
        w_perm = keep.tile([P, T, N], BF16, name="w_perm", align_bytes=64)
        for t in range(2):
            w_permute(t)
        for h in range(2):
            ps = bank("e")
            for tt in range(2):
                t = 2 * h + tt
                for u in range(2):
                    o = (2 * tt + u) * P
                    nc.tensor.transpose(ps[:, o:o + P], words[:, 256 * t + u:256 * (t + 1):2], ident[:])
            dst = w_g[:].bitcast(F32)[:, N * h:N * (h + 1)].rearrange("p (t r u) -> p t r u", t=2, u=2)
            src = ps[:].rearrange("p (t u r) -> p t r u", t=2, u=2)
            if h == 0:
                nc.vector.tensor_copy(out=dst, in_=src)
            else:
                nc.scalar.copy(out=dst, in_=src)
        c_g = {}
        c_q = {}
        v_g = {}
        v_q = {}
        y_acc = []
        for t in range(T):
            ya = keep.tile([P, N], F32, name="y_acc%d" % t)
            y_acc.append(ya)

        def c_interleave(k, t, eng):
            if k not in c_g:
                cg = ring.tile([P, 4 * N], BF16, name="c_g", tag="c_g", align_bytes=64)
                c_g[k] = cg
            dst = c_g[k][:].rearrange("p (t q j) -> p q t j", t=T, j=4)[:, 32 * t:32 * t + 32]
            src = c_raw[k][:].rearrange("p j (q t) -> p q t j", t=T)[:, 32 * t:32 * t + 32]
            if eng == "v":
                for h in range(2):
                    nc.vector.tensor_copy(out=dst[:, :, 2 * h:2 * h + 2], in_=src[:, :, 2 * h:2 * h + 2])
            elif eng == "g":
                nc.gpsimd.tensor_scalar(dst, src, 1.0, 0.0, op0=ALU.mult, op1=ALU.add)
            else:
                nc.scalar.copy(out=dst, in_=src)

        def c_quantize(k, h):
            if k not in c_q:
                cc = ring.tile([P, N], U32, name="c_codes", tag="c_codes", align_bytes=64)
                cs = ring.tile([P, N], U8, name="c_scales", tag="c_scales", align_bytes=64)
                c_q[k] = (cc, cs)
            cols = slice(256 * h, 256 * (h + 1))
            nc.vector.quantize_mx(out=c_q[k][0][:, cols].bitcast(FP8X4), scales=c_q[k][1][:, cols],
                                  in_=c_g[k][:, 1024 * h:1024 * (h + 1)])

        def mm(ps, lhs, lcols, rhs, rcols, start=True, stop=True):
            nc.tensor.matmul_mx(
                out=ps,
                lhsT=lhs[0][:, lcols].bitcast(FP8X4), lhsT_scale=lhs[1][:, lcols],
                rhs=rhs[0][:, rcols].bitcast(FP8X4), rhs_scale=rhs[1][:, rcols],
                start=start, stop=stop)

        wq = (w_codes, w_scales)
        full = slice(0, N)

        def blk(t):
            return slice(P * t, P * (t + 1))

        vt_ps = {}
        v_ps = {}
        e_ps = {}

        def vt_mm(i):
            k, g = divmod(i, T)
            ps = bank("vt")
            for t in range(T):
                mm(ps[:, blk(t)], c_q[k], blk(t), wq, blk(g))
            vt_ps[i] = ps

        def vt_out(i):
            k, g = divmod(i, T)
            if k not in v_g:
                vg = ring.tile([P, 4 * N], BF16, name="v_g", tag="v_g", align_bytes=64)
                v_g[k] = vg
            nc.scalar.copy(out=v_g[k][:, N * g:N * (g + 1)].rearrange("p (i t) -> p i t", t=T),
                           in_=vt_ps[i][:].rearrange("p (t i) -> p i t", t=T))

        def v_quantize(k, h):
            if h == 0:
                vc = ring.tile([P, N], U32, name="v_codes", tag="v_codes", align_bytes=64)
                vs = ring.tile([P, N], U8, name="v_scales", tag="v_scales", align_bytes=64)
                v_q[k] = (vc, vs)
            cols = slice(256 * h, 256 * (h + 1))
            nc.vector.quantize_mx(out=v_q[k][0][:, cols].bitcast(FP8X4), scales=v_q[k][1][:, cols],
                                  in_=v_g[k][:, 1024 * h:1024 * (h + 1)])

        def d_mm(j):
            k, t = divmod(j, T)
            ps = bank("v")
            mm(ps[:], wq, blk(t), c_q[k], full)
            v_ps[j] = ps

        def d_out(j):
            k, t = divmod(j, T)
            junk = ring.tile([P, N], F32, name="junk", tag="junk")
            nc.vector.scalar_tensor_tensor(
                out=junk[:], in0=v_ps[j][:], scalar=1.0, in1=w_perm[:, t, :],
                op0=ALU.mult, op1=ALU.mult, accum_out=d_all[:, t, k:k + 1])

        def e_mm(e):
            k, t = divmod(e, T)
            ps = bank("e")
            mm(ps[:], v_q[k], blk(t), wq, full, True, False)
            mm(ps[:], wq, blk(t), v_q[k], full, False, True)
            e_ps[e] = ps

        def e_out(e):
            k, t = divmod(e, T)
            ps = e_ps[e]
            dcol = d_all[:, t, k:k + 1]
            if t in SY[k]:
                tmp = y_acc[t]
                if k > 0:
                    tmp = ring.tile([P, N], F32, name="y_tmp", tag="y_tmp")
                nc.scalar.activation(out=tmp[:], in_=ps[:], func=ACT.Copy, scale=dcol)
                if k > 0:
                    nc.gpsimd.tensor_tensor(out=y_acc[t][:], in0=y_acc[t][:], in1=tmp[:], op=ALU.add)
            elif k == 0:
                nc.vector.tensor_scalar_mul(y_acc[t][:], ps[:], dcol)
            else:
                nc.vector.scalar_tensor_tensor(out=y_acc[t][:], in0=ps[:], scalar=dcol, in1=y_acc[t][:],
                                               op0=ALU.mult, op1=ALU.add)

        tail = {}
        z_ps = {}
        zz = {}
        den = {}
        gg = {}
        gl = {}
        w_y = {}
        p_y = {}

        split_a = keep.tile([P, T, P], BF16, name="split_a", align_bytes=64)
        split_b = keep.tile([P, T, P], BF16, name="split_b", align_bytes=64)
        nc.gpsimd.memset(split_a[:], 0.0)
        nc.gpsimd.memset(split_b[:], 0.0)

        def d_split():
            ones3 = [P, T, 3, KM]
            d = d_all[:]
            av = split_a[:, :, 0:9 * KM].rearrange("p t (a b k) -> p t a b k", a=3, b=3)
            bv = split_b[:, :, 0:9 * KM].rearrange("p t (a b k) -> p t a b k", a=3, b=3)
            rest = d
            for a in range(3):
                nc.gpsimd.tensor_scalar(av[:, :, a], rest.unsqueeze(2).to_broadcast(ones3), 1.0, 0.0, op0=ALU.mult, op1=ALU.add)
                if a < 2:
                    r = keep.tile([P, T, KM], F32, name="d_rest%d" % a)
                    nc.gpsimd.tensor_tensor(out=r[:], in0=rest, in1=av[:, :, a, 0, :], op=ALU.subtract)
                    rest = r[:]
            for a in range(3):
                nc.gpsimd.tensor_scalar(bv[:, :, :, a, :], av[:, :, a], 1.0, 0.0, op0=ALU.mult, op1=ALU.add)
            d2 = keep.tile([P, T, KM], F32, name="d2")
            nc.gpsimd.tensor_tensor(out=d2[:], in0=d, in1=d, op=ALU.mult)
            tail["d2"] = d2

        def zd_pass():
            zd = keep.tile([P, T], F32, name="zd")
            zs = keep.tile([P, T], F32, name="zs")
            ys = keep.tile([P, T], F32, name="ys")
            nc.vector.tensor_reduce(out=zd[:], in_=tail["d2"][:], axis=AX.X, op=ALU.add)
            nc.gpsimd.tensor_scalar(zs[:], zd[:], 1.21, 0.0, op0=ALU.mult, op1=ALU.add)
            nc.gpsimd.tensor_scalar(ys[:], zd[:], -1.1, 0.0, op0=ALU.mult, op1=ALU.add)
            tail["zd"], tail["zs"], tail["ys"] = zd, zs, ys

        def d_turn():
            assert "d2" in tail
            for name, src in (("at", split_a), ("bt", split_b)):
                ps = psum.tile([P, N], BF16, name="ps_" + name, tag=TBANK[name], bufs=BANKS[TBANK[name]])
                for t in range(T):
                    nc.tensor.transpose(ps[:, blk(t)], src[:, t, :], ident16[:])
                tail[name + "_ps"] = ps

        def d_copy():
            for name, eng in (("at", nc.vector.tensor_copy), ("bt", nc.scalar.copy)):
                s = keep.tile([P, N], BF16, name=name, align_bytes=64)
                eng(out=s[:], in_=tail[name + "_ps"][:])
                tail[name] = s

        def zdb_pass():
            ps = bank("v")
            for t in range(T):
                nc.tensor.matmul(ps[:, blk(t)], lhsT=tail["zd"][:, t:t + 1].to_broadcast([P, P]), rhs=ident[:],
                                 start=True, stop=True)
            tail["zdb"] = ps

        def z_pass(t):
            ps = bank(ZBANK[t])
            nc.tensor.matmul(ps[:], lhsT=tail["at"][:, blk(t)], rhs=tail["bt"][:], start=True, stop=True)
            z_ps[t] = ps

        def zz_pass(t):
            a = keep.tile([P, N], F32, name="zz%d" % t)
            nc.scalar.activation(out=a[:, P * t:], in_=z_ps[t][:, P * t:], func=ACT.Square)
            zz[t] = a

        def den_pass(t):
            a = keep.tile([P, N], F32, name="den%d" % t)
            nc.vector.scalar_tensor_tensor(out=a[:, P * t:], in0=tail["zdb"][:, P * t:], scalar=tail["zs"][:, t:t + 1],
                                           in1=zz[t][:, P * t:], op0=ALU.mult, op1=ALU.subtract)
            den[t] = a

        def gg_pass(t):
            r = keep.tile([P, N], F32, name="rs%d" % t)
            nc.scalar.activation(out=r[:, P * t:], in_=den[t][:, P * t:], func=ACT.Abs_reciprocal_sqrt, scale=2.0)
            a = keep.tile([P, N], F32, name="gg%d" % t)
            nc.scalar.activation(out=a[:, P * t:], in_=r[:, P * t:], func=ACT.Square)
            nc.gpsimd.affine_select(out=a[:, blk(t)], in_=a[:, blk(t)], pattern=[[1, P]], compare_op=ALU.not_equal,
                                    fill=0.0, base=0, channel_multiplier=-1)
            gg[t] = a

        def gl_pass(t):
            if t == 2:
                ps, o = gl[1][0], P
            else:
                ps, o = bank("e" if t == 1 else "v"), 0
            for t2 in range(t):
                nc.tensor.transpose(ps[:, o + P * t2:o + P * t2 + P], gg[t2][:, blk(t)], ident[:])
            gl[t] = (ps, o)

        def w_pass(t):
            a = keep.tile([P, N], F32, name="w_y%d" % t)
            eng = nc.gpsimd if t in WG else nc.vector
            eng.tensor_tensor(out=a[:, P * t:], in0=y_acc[t][:, P * t:], in1=gg[t][:, P * t:], op=ALU.mult)
            if t > 0:
                ps, o = gl[t]
                nc.vector.tensor_tensor(out=a[:, :P * t], in0=ps[:, o:o + P * t], in1=y_acc[t][:, :P * t], op=ALU.mult)
            w_y[t] = a

        def p_pass(t):
            a = keep.tile([P, N], F32, name="p_y%d" % t)
            nc.vector.tensor_tensor(out=a[:], in0=z_ps[t][:], in1=w_y[t][:], op=ALU.mult)
            p_y[t] = a

        for t in range(T):
            c_interleave(0, t, "v" if t < C0 else "s")
        nc.vector.quantize_mx(out=w_codes[:].bitcast(FP8X4), scales=w_scales[:], in_=w_g[:])
        c_quantize(0, 0)
        c_quantize(0, 1)
        w_permute(2)
        w_permute(3)
        i0 = min(LD, T - max(QC))
        for n in range(T, LC + i0):
            c_interleave(n // T, n % T, "v" if n in CVEC else "g" if n in CGPS else "s")

        END = T * KM
        assert all(WT[t] >= t - T and PT[t] >= WT[t] for t in range(T))
        for i in range(i0, END + LE + 4):
            e = i - LE
            j = i - LD
            vt_on, e_on, d_on = 0 <= i < END, 0 <= e < END, 0 <= j < END
            for what in PEORD:
                if what == "vt" and vt_on:
                    vt_mm(i)
                if what == "e" and e_on:
                    e_mm(e)
                if what == "d" and d_on:
                    d_mm(j)
            s_y = e_on and (e % T) in SY[e // T]
            for what in SORD:
                if what == "vt" and vt_on:
                    vt_out(i)
                if what == "y" and s_y:
                    e_out(e)
                n = i + LC
                if what == "c" and T <= n < END and n >= LC + i0 and n not in CVEC:
                    c_interleave(n // T, n % T, "g" if n in CGPS else "s")
            for what in VORD:
                if what == "y" and e_on and not s_y:
                    e_out(e)
                if what == "d" and d_on:
                    d_out(j)
                n = i + LC
                if what == "c" and T <= n < END and n in CVEC:
                    c_interleave(n // T, n % T, "v")
                if what == "qc":
                    for h in range(2):
                        n = i + QC[h]
                        if n % T == 0 and T <= n < END:
                            c_quantize(n // T, h)
                if what == "qv":
                    for h in range(2):
                        n = i - QV[h]
                        if n % T == 0 and 0 <= n < END:
                            v_quantize(n // T, h)
            if i == DS:
                d_split()
            if i == RD:
                zd_pass()
            if i == DT:
                d_turn()
            if i == DC:
                d_copy()
            if i == ZB:
                zdb_pass()
            for t in range(T):
                if i == ZT[t]:
                    z_pass(t)
                if i == ZZ[t]:
                    zz_pass(t)
                if i == DN[t]:
                    den_pass(t)
                if i == GT[t]:
                    gg_pass(t)
            for t in range(1, T):
                if i == GL[t]:
                    gl_pass(t)
            for t in range(T):
                if e == END + WT[t]:
                    w_pass(t)
            for t in range(T):
                if e == END + PT[t]:
                    p_pass(t)

        ty_ps = []
        u_all = keep.tile([P, T, N], F32, name="u_all")
        u_g = keep.tile([P, 4 * N], BF16, name="u_g", align_bytes=64)
        o_codes = keep.tile([P, N], U32, name="o_codes", align_bytes=64)
        o_scales = keep.tile([P, N], U8, name="o_scales", align_bytes=64)
        o0 = out_0.rearrange("(p t) m -> p t m", t=T)
        o1 = out_1.rearrange("g p m t -> (g p) (m t)").bitcast(I32)
        o2 = out_2.rearrange("g q m -> (g q) m").bitcast(I32)

        for t in range(T):
            ps = bank("e" if t < 3 else "v")
            for t2 in range(T):
                nc.tensor.transpose(ps[:, blk(t2)], w_y[t2][:, blk(t)], ident[:])
            ty_ps.append(ps)
        for h in range(2):
            cols = slice(256 * h, 256 * (h + 1))
            qs = slice(64 * h, 64 * (h + 1))
            for t in range(T):
                nc.vector.scalar_tensor_tensor(out=u_all[:, t, cols].rearrange("p (q s) -> p q s", s=T),
                                               in0=ty_ps[t][:].rearrange("p (s q) -> p q s", s=T)[:, qs],
                                               scalar=tail["ys"][:, t:t + 1],
                                               in1=p_y[t][:].rearrange("p (s q) -> p q s", s=T)[:, qs],
                                               op0=ALU.mult, op1=ALU.add)
            nc.sync.dma_start(out=o0[:, :, cols], in_=u_all[:, :, cols])
            dst = u_g[:, 1024 * h:1024 * (h + 1)].rearrange("p (m t) -> p m t", t=T)
            src = u_all[:, :, cols].rearrange("p t m -> p m t")
            if h == 0:
                nc.scalar.copy(out=dst, in_=src)
            else:
                nc.vector.tensor_copy(out=dst, in_=src)
        for h in range(2):
            cols = slice(256 * h, 256 * (h + 1))
            nc.vector.quantize_mx(out=o_codes[:, cols].bitcast(FP8X4), scales=o_scales[:, cols],
                                  in_=u_g[:, 1024 * h:1024 * (h + 1)])
            nc.sync.dma_start(out=o1[:, cols], in_=o_codes[:, cols].bitcast(I32))
        for b in range(4):
            eng = (nc.scalar, nc.gpsimd, nc.scalar, nc.sync)[b]
            eng.dma_start(out=o2[4 * b:4 * b + 4, :], in_=o_scales[32 * b:32 * b + 4, :].bitcast(I32))
